import numpy as np
import ml_dtypes


def mxq(x, axis, fmt="e4m3"):
    dtype, down = {"e4m3": (ml_dtypes.float8_e4m3fn, 7), "e5m2": (ml_dtypes.float8_e5m2, 14)}[fmt]
    v = np.moveaxis(np.asarray(x, np.float32).astype(ml_dtypes.bfloat16).astype(np.float64), axis, -1)
    blocks = v.reshape(v.shape[:-1] + (-1, 32))
    amax = np.abs(blocks).max(-1, keepdims=True)
    byte = np.maximum(np.where(amax > 0, np.frexp(amax)[1] - 1 + 127, 0) - down, 1)
    scale = np.exp2(byte - 127.0)
    codes = (blocks / scale).astype(np.float32).astype(dtype).astype(np.float64)
    return np.moveaxis((codes * scale).reshape(v.shape), -1, axis)


WIDE = False


def mx_kscale(k):
    if not WIDE:
        return np.ones(k)
    levels = np.array([10, -10, 5, -5, 0])
    if k % 512:
        return np.exp2(np.random.permutation(np.resize(levels, k // 32))).repeat(32)
    a = np.empty((k // 512, 16))
    for p in range(k // 512):
        a[p, :8] = np.random.permutation(np.resize(levels, 8))
        for g in range(8):
            far = levels[np.abs(levels - a[p, g]) >= 10]
            a[p, g + 8] = far[np.random.randint(len(far))]
    return np.exp2(a.ravel()).repeat(32)


def f64(x):
    return np.asarray(x).astype(np.float64)


def striped(idx):
    return np.tile(np.asarray(idx).reshape(-1, 16).T, (8, 1)).astype(np.uint16)


def unstriped(offs):
    return offs[:16].T.reshape(-1).astype(np.int64)


E2M1 = np.array([0.0, 0.5, 1.0, 1.5, 2.0, 3.0, 4.0, 6.0, -0.0, -0.5, -1.0, -1.5, -2.0, -3.0, -4.0, -6.0])


def pack_weight(w, fmt):
    k, n = w.shape
    w = f64(np.asarray(w, np.float32).astype(ml_dtypes.bfloat16)).reshape(k // 32, 32, n)
    amax = np.abs(w).max(1)
    if fmt == "e4m3":
        byte = np.frexp(amax)[1] - 1 + 127 - 7
    else:
        mant, ex = np.frexp(amax / 6.0)
        byte = np.where(mant > 0.5, ex, ex - 1) + 127
    byte = np.clip(np.where(amax > 0, byte, 1), 1, 254)
    scaled = (w * np.exp2(127.0 - byte)[:, None, :]).reshape(k, n).astype(np.float32)
    by_word = np.ascontiguousarray(scaled.reshape(k // 512, 128, 4, n).transpose(0, 1, 3, 2))
    if fmt == "e4m3":
        words = by_word.astype(ml_dtypes.float8_e4m3fn).view(np.uint8)
    else:
        c = by_word.astype(ml_dtypes.float4_e2m1fn).view(np.uint8) & 0xF
        words = (c[..., 0::2] | (c[..., 1::2] << 4)).reshape(k // 512, 128, 2 * n)
    return np.ascontiguousarray(words), np.ascontiguousarray(byte.astype(np.uint8).reshape(k // 512, 16, n))


def unpack_weight(words, scales, fmt):
    g, _, n = scales.shape
    words = np.ascontiguousarray(words).reshape(g, 128, n, -1)
    if fmt == "e4m3":
        vals = words.view(ml_dtypes.float8_e4m3fn).astype(np.float64)
    else:
        nib = np.empty((g, 128, n, 4), np.uint8)
        nib[..., 0::2] = words & 0xF
        nib[..., 1::2] = words >> 4
        vals = E2M1[nib]
    vals = vals * np.repeat(np.exp2(scales.astype(np.float64) - 127.0), 8, axis=1)[..., None]
    return vals.transpose(0, 1, 3, 2).reshape(g * 512, n)


D, E, T, I, Q = 512, 512, 2048, 512, 128


def setup_inputs():
    n = np.random.standard_normal
    idx = np.random.permutation(T)[:I]
    fd = mx_kscale(D)
    fe = mx_kscale(E)
    keysp = pack_weight(n((D, T)) / fd[:, None], "e2m1")
    valsp = pack_weight(n((E, T)) / fe[:, None], "e2m1")
    return {
        "query": (n((D, Q)) * 0.6 / np.sqrt(D) * fd[:, None]).astype(np.float32),
        "keys_words": keysp[0],
        "keys_scales": keysp[1],
        "age": np.tile(np.random.uniform(0.0, 2.0, T), (128, 1)).astype(np.float32),
        "rate": (np.random.uniform(0.3, 1.2, (Q, 1))).astype(np.float32),
        "reserve": (np.random.uniform(20.0, 100.0, (Q, 1))).astype(np.float32),
        "gout": (n((E, Q)) * 1 / np.sqrt(E) * fe[:, None]).astype(np.float32),
        "vals_words": valsp[0],
        "vals_scales": valsp[1],
        "size": (np.random.uniform(0.5, 2.0, (1, I))).astype(np.float32),
        "base": (0.5 * n((Q, I))).astype(np.float32),
        "offs": striped(idx),
    }


def reference(query, keys_words, keys_scales, age, rate, reserve, gout, vals_words, vals_scales, size, base, offs):
    idx = unstriped(offs)
    keysu = unpack_weight(keys_words, keys_scales, "e2m1")
    valsu = unpack_weight(vals_words, vals_scales, "e2m1")
    queryq = mxq(f64(query), 0, "e4m3")
    keysidxg = keysu[:, idx]
    a = queryq.T @ keysidxg
    p = np.exp(a - f64(age)[:1][:, idx] * f64(rate))
    z = np.sum(p, axis=1, keepdims=True) + f64(reserve)
    goutq = mxq(f64(gout), 0, "e4m3")
    valsidxg = valsu[:, idx]
    c0 = goutq.T @ valsidxg
    dz = np.sum(c0 * p * f64(size) / np.square(z) * (-1.0), axis=1, keepdims=True)
    dp = c0 / z * f64(size) + dz
    da = dp * p
    hda = da * 512.0 * 2.0 * 512.0
    hdp = hda * p
    hdz = np.sum(hdp, axis=1, keepdims=True)
    hz = np.sum(hdp * f64(size) * c0 / np.square(z) * (-1.0), axis=1, keepdims=True) + np.sum(hdz * (-1.0) * c0 * p * f64(size) / np.square(np.square(z)) * (-1.0), axis=1, keepdims=True) * z * 2.0
    hp = hda * dp + hdz * (-1.0) / np.square(z) * c0 * f64(size) + hz
    ha = hp * p
    y = ha + f64(base)
    return y

@@ -1,0 +1,202 @@
+import math
+from contextlib import ExitStack
+
+import concourse.mybir as mybir
+from concourse.masks import make_identity
+
+D, E, T, I, Q = 512, 512, 2048, 512, 128
+FLOPS = 2 * Q * I * (D + E)
+
+F32 = mybir.dt.float32
+BF16 = mybir.dt.bfloat16
+I32 = mybir.dt.int32
+U32 = mybir.dt.uint32
+U16 = mybir.dt.uint16
+U8 = mybir.dt.uint8
+FP8X4 = mybir.dt.float8_e4m3fn_x4
+FP4X4 = mybir.dt.float4_e2m1fn_x4
+ALU = mybir.AluOpType
+ACT = mybir.ActivationFunctionType
+
+P = 128
+PACK = 4
+BLOCKS = I // P
+AGE_ROW = P - 1
+ROOT_K = math.sqrt(512.0 * 2.0 * 512.0)
+
+
+def tile_attend_gpfadereserve_kernel(
+    tc, query, keys_words, keys_scales, age, rate, reserve, gout, vals_words, vals_scales, size, base, offs, out
+):
+    nc = tc.nc
+    with ExitStack() as ctx:
+        sb = ctx.enter_context(tc.tile_pool(name="sb", bufs=1))
+        ps = ctx.enter_context(tc.psum_pool(name="ps", bufs=1))
+
+        def tile(name, shape, dtype):
+            return sb.tile(shape, dtype, name=name, align_bytes=64)
+
+        def bank(name, shape):
+            return ps.tile(shape, F32, name=name)
+
+        def load_words(name, words):
+            window = tile(name, [P, T], U16)
+            nc.sync.dma_start(window[:].bitcast(I32), words[0].bitcast(I32))
+            return window
+
+        def load_scale_rows(window, scales):
+            for f in range(4):
+                nc.sync.dma_start(window[f:P:32, :].bitcast(I32), scales[0, f:16:4, :].bitcast(I32))
+
+        def load_rows(name, rows):
+            raw = tile(name, [P, PACK, Q], F32)
+            nc.sync.dma_start(raw[:], rows.rearrange("(p j) w -> p j w", j=PACK))
+            return raw
+
+        def quantise(name, raw):
+            grouped = tile(name + "_bf16", [P, Q, PACK], BF16)
+            nc.scalar.copy(
+                grouped[:].rearrange("p (c i) t -> p c t i", i=4),
+                raw[:].rearrange("p t (c i) -> p c t i", i=4),
+            )
+            codes = tile(name + "_codes", [P, Q], U32)
+            plane = tile(name + "_plane", [P, Q], U8)
+            nc.vector.quantize_mx(codes[:].bitcast(FP8X4), plane[:], grouped[:].rearrange("p w t -> p (w t)"))
+            return codes, plane
+
+        def gather(name, window, dtype):
+            picked = tile(name, [P, I], dtype)
+            nc.vector.tensor_copy(picked[:], window[:].indirect(offsets[:]))
+            return picked
+
+        key_scale_window = tile("key_scale_window", [P, T], U8)
+        val_scale_window = tile("val_scale_window", [P, T], U8)
+        age_window = tile("age_window", [P, T], F32)
+        nc.vector.memset(key_scale_window[:].bitcast(I32), 0)
+        nc.vector.memset(age_window[0:AGE_ROW, :], 0.0)
+        nc.vector.memset(val_scale_window[:].bitcast(I32), 0)
+
+        warm_in = tile("warm_in", [P, 1], F32)
+        warm_out = tile("warm_out", [P, 1], F32)
+        nc.gpsimd.memset(warm_in[:], 0.0)
+        nc.scalar.activation(warm_out[:], warm_in[:], ACT.Exp)
+        ident = tile("ident", [P, P], F32)
+        make_identity(nc, ident[:])
+
+        offsets = sb.tile([P, I // 16], U16, name="offsets")
+        nc.sync.dma_start(offsets[:], offs)
+        nc.sync.dma_start(age_window[AGE_ROW:P, :], age[0:1, :])
+        key_window = load_words("key_window", keys_words)
+        rate_col = tile("rate_col", [P, 1], F32)
+        nc.sync.dma_start(rate_col[:], rate)
+        load_scale_rows(key_scale_window, keys_scales)
+        query_raw = load_rows("query_raw", query)
+        val_window = load_words("val_window", vals_words)
+        load_scale_rows(val_scale_window, vals_scales)
+        gout_raw = load_rows("gout_raw", gout)
+        size_cols = tile("size_cols", [P, 4], F32)
+        nc.sync.dma_start(size_cols[:], size[0].rearrange("(p j) -> p j", j=4))
+        reserve_col = tile("reserve_col", [P, 1], F32)
+        nc.sync.dma_start(reserve_col[:], reserve)
+        base_sb = tile("base_sb", [P, I], F32)
+        nc.sync.dma_start(base_sb[:], base)
+
+        age_picked = gather("age_picked", age_window, F32)
+        rate_rows = bank("rate_rows", [P, Q])
+        nc.tensor.transpose(rate_rows[:], rate_col[:].to_broadcast([P, P]), ident[:])
+        age_turned = bank("age_turned", [P, BLOCKS, P])
+        for j in range(BLOCKS):
+            nc.tensor.transpose(age_turned[:, j, :], age_picked[:, j * P : (j + 1) * P], ident[:])
+        neg_age = tile("neg_age", [P, BLOCKS], F32)
+        nc.scalar.activation(neg_age[:], age_turned[:, :, AGE_ROW], ACT.Copy, scale=-1.0)
+        fade_t = tile("fade_t", [P, BLOCKS, Q], F32)
+        for j in range(BLOCKS):
+            nc.scalar.activation(fade_t[:, j, :], rate_rows[:], ACT.Copy, scale=neg_age[:, j : j + 1])
+        exponent = bank("exponent", [P, BLOCKS, P])
+        for j in range(BLOCKS):
+            nc.tensor.matmul(exponent[:, j, :], fade_t[:, j, :], ident[:], start=(j == 0), stop=False, is_transpose=True)
+
+        key_words = gather("key_words", key_window, U16)
+        key_plane = gather("key_plane", key_scale_window, U8)
+        query_codes, query_plane = quantise("query", query_raw)
+        score_t = tile("score_t", [P, BLOCKS, Q], F32)
+        for h in range(2):
+            score_bank = bank("score_bank%d" % h, [P, 2, Q])
+            for u in range(2):
+                cols = slice((2 * h + u) * P, (2 * h + u + 1) * P)
+                nc.tensor.matmul_mx(
+                    score_bank[:, u, :],
+                    lhsT=key_words[:, cols].bitcast(FP4X4),
+                    lhsT_scale=key_plane[:, cols],
+                    rhs=query_codes[:].bitcast(FP8X4),
+                    rhs_scale=query_plane[:],
+                    start=True,
+                    stop=True,
+                )
+            nc.scalar.copy(score_t[:, 2 * h : 2 * h + 2, :], score_bank[:])
+        for j in range(BLOCKS):
+            nc.tensor.matmul(
+                exponent[:, j, :], score_t[:, j, :], ident[:], start=False, stop=(j == BLOCKS - 1), is_transpose=True
+            )
+        p = tile("p", [P, I], F32)
+        p_sum = tile("p_sum", [P, 1], F32)
+        nc.scalar.activation(p[:], exponent[:].rearrange("q j s -> q (j s)"), ACT.Exp, accum_out=p_sum[:])
+
+        val_words = gather("val_words", val_window, U16)
+        gout_codes, gout_plane = quantise("gout", gout_raw)
+        val_plane = gather("val_plane", val_scale_window, U8)
+        c0 = bank("c0", [P, I])
+        nc.tensor.matmul_mx(
+            c0[:],
+            lhsT=gout_codes[:].bitcast(FP8X4),
+            lhsT_scale=gout_plane[:],
+            rhs=val_words[:].bitcast(FP4X4),
+            rhs_scale=val_plane[:],
+            start=True,
+            stop=True,
+        )
+        size_rows = bank("size_rows", [P, 4, P])
+        for j in range(4):
+            nc.tensor.transpose(size_rows[:, j, :], size_cols[:, j : j + 1].to_broadcast([P, P]), ident[:])
+
+        neg_z = tile("neg_z", [P, 1], F32)
+        nc.vector.tensor_scalar(neg_z[:], p_sum[:], reserve_col[:], -1.0, ALU.add, ALU.mult)
+        p_size = tile("p_size", [P, I], F32)
+        nc.vector.tensor_tensor(
+            p_size[:].rearrange("q (s j) -> q s j", j=4),
+            p[:].rearrange("q (s j) -> q s j", j=4),
+            size_rows[:].rearrange("q j s -> q s j"),
+            ALU.mult,
+        )
+        neg_r = tile("neg_r", [P, 1], F32)
+        nc.vector.reciprocal(neg_r[:], neg_z[:])
+        neg_s = tile("neg_s", [P, I], F32)
+        nc.scalar.activation(neg_s[:], p[:], ACT.Copy, scale=neg_r[:])
+        v = tile("v", [P, I], F32)
+        v_sum = tile("v_sum", [P, 1], F32)
+        nc.vector.scalar_tensor_tensor(v[:], p_size[:], 1.0, c0[:], ALU.mult, ALU.mult, accum_out=v_sum[:])
+        gain = tile("gain", [P, 1], F32)
+        nc.vector.tensor_scalar(gain[:], neg_r[:], ROOT_K, None, ALU.mult)
+        half_gain = tile("half_gain", [P, 1], F32)
+        nc.vector.tensor_scalar(half_gain[:], neg_r[:], 0.5 * ROOT_K, None, ALU.mult)
+        t = tile("t", [P, I], F32)
+        nc.vector.scalar_tensor_tensor(t[:], neg_s[:], v_sum[:], v[:], ALU.mult, ALU.add)
+        squares = tile("squares", [P, I], F32)
+        square_sum = tile("square_sum", [P, 1], F32)
+        nc.scalar.activation(squares[:], t[:], ACT.Square, scale=gain[:], accum_out=square_sum[:])
+        cross = tile("cross", [P, I], F32)
+        shift = tile("shift", [P, 1], F32)
+        nc.vector.scalar_tensor_tensor(cross[:], t[:], half_gain[:], neg_s[:], ALU.mult, ALU.mult, accum_out=shift[:])
+        shifted = tile("shifted", [P, I], F32)
+        nc.scalar.activation(shifted[:], t[:], ACT.Square, scale=gain[:], bias=shift[:])
+        linear = tile("linear", [P, I], F32)
+        nc.vector.scalar_tensor_tensor(linear[:], neg_s[:], square_sum[:], base_sb[:], ALU.mult, ALU.add)
+        shift_sq = tile("shift_sq", [P, 1], F32)
+        nc.vector.tensor_tensor(shift_sq[:], shift[:], shift[:], ALU.mult)
+        for h in range(2):
+            cols = slice(h * I // 2, (h + 1) * I // 2)
+            result = tile("result%d" % h, [P, I // 2], F32)
+            nc.vector.scalar_tensor_tensor(
+                result[:], shifted[:, cols], shift_sq[:], linear[:, cols], ALU.subtract, ALU.add
+            )
+            nc.sync.dma_start(out[:, cols], result[:])

@@ -21,6 +21,7 @@ ACT = mybir.ActivationFunctionType
 P = 128
 PACK = 4
 BLOCKS = I // P
+HALF = I // 2
 AGE_ROW = P - 1
 ROOT_K = math.sqrt(512.0 * 2.0 * 512.0)
 
@@ -33,11 +34,11 @@ def tile_attend_gpfadereserve_kernel(
         sb = ctx.enter_context(tc.tile_pool(name="sb", bufs=1))
         ps = ctx.enter_context(tc.psum_pool(name="ps", bufs=1))
 
-        def tile(name, shape, dtype):
-            return sb.tile(shape, dtype, name=name, align_bytes=64)
+        def tile(name, shape, dtype, tag=None):
+            return sb.tile(shape, dtype, name=name, tag=tag or name, align_bytes=64)
 
-        def bank(name, shape):
-            return ps.tile(shape, F32, name=name)
+        def bank(name, shape, tag=None):
+            return ps.tile(shape, F32, name=name, tag=tag or name)
 
         def load_words(name, words):
             window = tile(name, [P, T], U16)
@@ -53,12 +54,15 @@ def tile_attend_gpfadereserve_kernel(
             nc.sync.dma_start(raw[:], rows.rearrange("(p j) w -> p j w", j=PACK))
             return raw
 
-        def quantise(name, raw):
+        def interleave(name, raw):
             grouped = tile(name + "_bf16", [P, Q, PACK], BF16)
             nc.scalar.copy(
                 grouped[:].rearrange("p (c i) t -> p c t i", i=4),
                 raw[:].rearrange("p t (c i) -> p c t i", i=4),
             )
+            return grouped
+
+        def quantise(name, grouped):
             codes = tile(name + "_codes", [P, Q], U32)
             plane = tile(name + "_plane", [P, Q], U8)
             nc.vector.quantize_mx(codes[:].bitcast(FP8X4), plane[:], grouped[:].rearrange("p w t -> p (w t)"))
@@ -76,6 +80,10 @@ def tile_attend_gpfadereserve_kernel(
         nc.vector.memset(age_window[0:AGE_ROW, :], 0.0)
         nc.vector.memset(val_scale_window[:].bitcast(I32), 0)
 
+        rate_col = tile("rate_col", [P, 1], F32)
+        nc.scalar.dma_start(rate_col[:], rate)
+        size_cols = tile("size_cols", [P, 4], F32)
+        nc.scalar.dma_start(size_cols[:], size[0].rearrange("(p j) -> p j", j=4))
         warm_in = tile("warm_in", [P, 1], F32)
         warm_out = tile("warm_out", [P, 1], F32)
         nc.gpsimd.memset(warm_in[:], 0.0)
@@ -87,19 +95,18 @@ def tile_attend_gpfadereserve_kernel(
         nc.sync.dma_start(offsets[:], offs)
         nc.sync.dma_start(age_window[AGE_ROW:P, :], age[0:1, :])
         key_window = load_words("key_window", keys_words)
-        rate_col = tile("rate_col", [P, 1], F32)
-        nc.sync.dma_start(rate_col[:], rate)
-        load_scale_rows(key_scale_window, keys_scales)
         query_raw = load_rows("query_raw", query)
+        load_scale_rows(key_scale_window, keys_scales)
+        gout_raw = load_rows("gout_raw", gout)
         val_window = load_words("val_window", vals_words)
         load_scale_rows(val_scale_window, vals_scales)
-        gout_raw = load_rows("gout_raw", gout)
-        size_cols = tile("size_cols", [P, 4], F32)
-        nc.sync.dma_start(size_cols[:], size[0].rearrange("(p j) -> p j", j=4))
         reserve_col = tile("reserve_col", [P, 1], F32)
         nc.sync.dma_start(reserve_col[:], reserve)
         base_sb = tile("base_sb", [P, I], F32)
         nc.sync.dma_start(base_sb[:], base)
+
+        query_bf16 = interleave("query", query_raw)
+        gout_bf16 = interleave("gout", gout_raw)
 
         age_picked = gather("age_picked", age_window, F32)
         rate_rows = bank("rate_rows", [P, Q])
@@ -107,20 +114,32 @@ def tile_attend_gpfadereserve_kernel(
         age_turned = bank("age_turned", [P, BLOCKS, P])
         for j in range(BLOCKS):
             nc.tensor.transpose(age_turned[:, j, :], age_picked[:, j * P : (j + 1) * P], ident[:])
-        neg_age = tile("neg_age", [P, BLOCKS], F32)
-        nc.scalar.activation(neg_age[:], age_turned[:, :, AGE_ROW], ACT.Copy, scale=-1.0)
-        fade_t = tile("fade_t", [P, BLOCKS, Q], F32)
+        size_rows = bank("size_rows", [P, 4, P])
+        for j in range(4):
+            nc.tensor.transpose(size_rows[:, j, :], size_cols[:, j : j + 1].to_broadcast([P, P]), ident[:])
+        fade_and_age = tile("fade_and_age", [P, BLOCKS * Q + BLOCKS], F32, tag="query_raw")
+        neg_age = fade_and_age[:, BLOCKS * Q :]
+        fade_t = fade_and_age[:, : BLOCKS * Q].rearrange("s (j q) -> s j q", j=BLOCKS)
+        nc.scalar.activation(neg_age, age_turned[:, :, AGE_ROW], ACT.Copy, scale=-1.0)
         for j in range(BLOCKS):
             nc.scalar.activation(fade_t[:, j, :], rate_rows[:], ACT.Copy, scale=neg_age[:, j : j + 1])
-        exponent = bank("exponent", [P, BLOCKS, P])
+        exponent = [bank("exponent%d" % h, [P, 2, P]) for h in range(2)]
         for j in range(BLOCKS):
-            nc.tensor.matmul(exponent[:, j, :], fade_t[:, j, :], ident[:], start=(j == 0), stop=False, is_transpose=True)
+            nc.tensor.matmul(
+                exponent[j // 2][:, j % 2, :], fade_t[:, j, :], ident[:], start=(j % 2 == 0), stop=False, is_transpose=True
+            )
 
         key_words = gather("key_words", key_window, U16)
-        key_plane = gather("key_plane", key_scale_window, U8)
-        query_codes, query_plane = quantise("query", query_raw)
-        score_t = tile("score_t", [P, BLOCKS, Q], F32)
+        query_codes, query_plane = quantise("query", query_bf16)
+        key_plane = tile("key_plane", [P, I], U8, tag="query_bf16")
+        score_t = tile("score_t", [P, BLOCKS, Q], F32, tag="gout_raw")
+        p = tile("p", [P, I], F32)
+        z = reserve_col
         for h in range(2):
+            half = slice(h * HALF, (h + 1) * HALF)
+            nc.vector.tensor_copy(
+                key_plane[:, half], key_scale_window[:].indirect(offsets[:, h * HALF // 16 : (h + 1) * HALF // 16])
+            )
             score_bank = bank("score_bank%d" % h, [P, 2, Q])
             for u in range(2):
                 cols = slice((2 * h + u) * P, (2 * h + u + 1) * P)
@@ -134,18 +153,20 @@ def tile_attend_gpfadereserve_kernel(
                     stop=True,
                 )
             nc.scalar.copy(score_t[:, 2 * h : 2 * h + 2, :], score_bank[:])
-        for j in range(BLOCKS):
-            nc.tensor.matmul(
-                exponent[:, j, :], score_t[:, j, :], ident[:], start=False, stop=(j == BLOCKS - 1), is_transpose=True
-            )
-        p = tile("p", [P, I], F32)
-        p_sum = tile("p_sum", [P, 1], F32)
-        nc.scalar.activation(p[:], exponent[:].rearrange("q j s -> q (j s)"), ACT.Exp, accum_out=p_sum[:])
+            for u in range(2):
+                nc.tensor.matmul(
+                    exponent[h][:, u, :], score_t[:, 2 * h + u, :], ident[:], start=False, stop=(u == 1), is_transpose=True
+                )
+            p_sum = tile("p_sum%d" % h, [P, 1], F32)
+            nc.scalar.activation(p[:, half], exponent[h][:].rearrange("q j s -> q (j s)"), ACT.Exp, accum_out=p_sum[:])
+            z_next = tile("z%d" % h, [P, 1], F32)
+            nc.scalar.activation(z_next[:], p_sum[:], ACT.Identity, bias=z[:])
+            z = z_next
 
         val_words = gather("val_words", val_window, U16)
-        gout_codes, gout_plane = quantise("gout", gout_raw)
+        gout_codes, gout_plane = quantise("gout", gout_bf16)
         val_plane = gather("val_plane", val_scale_window, U8)
-        c0 = bank("c0", [P, I])
+        c0 = bank("c0", [P, I], tag="exponent1")
         nc.tensor.matmul_mx(
             c0[:],
             lhsT=gout_codes[:].bitcast(FP8X4),
@@ -155,48 +176,43 @@ def tile_attend_gpfadereserve_kernel(
             start=True,
             stop=True,
         )
-        size_rows = bank("size_rows", [P, 4, P])
-        for j in range(4):
-            nc.tensor.transpose(size_rows[:, j, :], size_cols[:, j : j + 1].to_broadcast([P, P]), ident[:])
 
-        neg_z = tile("neg_z", [P, 1], F32)
-        nc.vector.tensor_scalar(neg_z[:], p_sum[:], reserve_col[:], -1.0, ALU.add, ALU.mult)
-        p_size = tile("p_size", [P, I], F32)
+        p_size_and_r = tile("p_size_and_r", [P, I + 1], F32, tag="val_scale_window")
+        p_size = p_size_and_r[:, :I]
+        r = p_size_and_r[:, I:]
         nc.vector.tensor_tensor(
-            p_size[:].rearrange("q (s j) -> q s j", j=4),
+            p_size.rearrange("q (s j) -> q s j", j=4),
             p[:].rearrange("q (s j) -> q s j", j=4),
             size_rows[:].rearrange("q j s -> q s j"),
             ALU.mult,
         )
-        neg_r = tile("neg_r", [P, 1], F32)
-        nc.vector.reciprocal(neg_r[:], neg_z[:])
-        neg_s = tile("neg_s", [P, I], F32)
-        nc.scalar.activation(neg_s[:], p[:], ACT.Copy, scale=neg_r[:])
+        nc.vector.reciprocal(r, z[:])
+        s = tile("s", [P, I], F32)
+        nc.scalar.activation(s[:], p[:], ACT.Copy, scale=r)
         v = tile("v", [P, I], F32)
         v_sum = tile("v_sum", [P, 1], F32)
-        nc.vector.scalar_tensor_tensor(v[:], p_size[:], 1.0, c0[:], ALU.mult, ALU.mult, accum_out=v_sum[:])
-        gain = tile("gain", [P, 1], F32)
-        nc.vector.tensor_scalar(gain[:], neg_r[:], ROOT_K, None, ALU.mult)
-        half_gain = tile("half_gain", [P, 1], F32)
-        nc.vector.tensor_scalar(half_gain[:], neg_r[:], 0.5 * ROOT_K, None, ALU.mult)
+        nc.vector.scalar_tensor_tensor(v[:], p_size, r, c0[:], ALU.mult, ALU.mult, accum_out=v_sum[:])
         t = tile("t", [P, I], F32)
-        nc.vector.scalar_tensor_tensor(t[:], neg_s[:], v_sum[:], v[:], ALU.mult, ALU.add)
+        nc.vector.scalar_tensor_tensor(t[:], s[:], v_sum[:], v[:], ALU.mult, ALU.subtract)
         squares = tile("squares", [P, I], F32)
         square_sum = tile("square_sum", [P, 1], F32)
-        nc.scalar.activation(squares[:], t[:], ACT.Square, scale=gain[:], accum_out=square_sum[:])
+        nc.scalar.activation(squares[:], t[:], ACT.Square, scale=ROOT_K, accum_out=square_sum[:])
         cross = tile("cross", [P, I], F32)
         shift = tile("shift", [P, 1], F32)
-        nc.vector.scalar_tensor_tensor(cross[:], t[:], half_gain[:], neg_s[:], ALU.mult, ALU.mult, accum_out=shift[:])
-        shifted = tile("shifted", [P, I], F32)
-        nc.scalar.activation(shifted[:], t[:], ACT.Square, scale=gain[:], bias=shift[:])
+        nc.vector.scalar_tensor_tensor(cross[:], t[:], -0.5 * ROOT_K, s[:], ALU.mult, ALU.mult, accum_out=shift[:])
+        halves = [slice(h * HALF, (h + 1) * HALF) for h in range(2)]
         linear = tile("linear", [P, I], F32)
-        nc.vector.scalar_tensor_tensor(linear[:], neg_s[:], square_sum[:], base_sb[:], ALU.mult, ALU.add)
-        shift_sq = tile("shift_sq", [P, 1], F32)
-        nc.vector.tensor_tensor(shift_sq[:], shift[:], shift[:], ALU.mult)
-        for h in range(2):
-            cols = slice(h * I // 2, (h + 1) * I // 2)
-            result = tile("result%d" % h, [P, I // 2], F32)
+        for half in halves:
             nc.vector.scalar_tensor_tensor(
-                result[:], shifted[:, cols], shift_sq[:], linear[:, cols], ALU.subtract, ALU.add
+                linear[:, half], s[:, half], square_sum[:], base_sb[:, half], ALU.mult, ALU.subtract
             )
-            nc.sync.dma_start(out[:, cols], result[:])
+        shift_sq = tile("shift_sq", [P, 1], F32)
+        nc.scalar.activation(shift_sq[:], shift[:], ACT.Square)
+        shifted = tile("shifted", [P, I], F32)
+        result = tile("result", [P, I], F32)
+        for half in halves:
+            nc.scalar.activation(shifted[:, half], t[:, half], ACT.Square, scale=ROOT_K, bias=shift[:])
+            nc.vector.scalar_tensor_tensor(
+                result[:, half], shifted[:, half], shift_sq[:], linear[:, half], ALU.subtract, ALU.subtract
+            )
+            nc.sync.dma_start(out[:, half], result[:, half])

import math
from contextlib import ExitStack

import concourse.mybir as mybir
from concourse.masks import make_identity

D, E, T, I, Q = 512, 512, 2048, 512, 128
FLOPS = 2 * Q * I * (D + E)

F32 = mybir.dt.float32
BF16 = mybir.dt.bfloat16
I32 = mybir.dt.int32
U32 = mybir.dt.uint32
U16 = mybir.dt.uint16
U8 = mybir.dt.uint8
FP8X4 = mybir.dt.float8_e4m3fn_x4
FP4X4 = mybir.dt.float4_e2m1fn_x4
ALU = mybir.AluOpType
ACT = mybir.ActivationFunctionType

P = 128
PACK = 4
BLOCKS = I // P
HALF = I // 2
AGE_ROW = P - 1
ROOT_K = math.sqrt(512.0 * 2.0 * 512.0)


def tile_attend_gpfadereserve_kernel(
    tc, query, keys_words, keys_scales, age, rate, reserve, gout, vals_words, vals_scales, size, base, offs, out
):
    nc = tc.nc
    with ExitStack() as ctx:
        sb = ctx.enter_context(tc.tile_pool(name="sb", bufs=1))
        ps = ctx.enter_context(tc.psum_pool(name="ps", bufs=1))

        def tile(name, shape, dtype, tag=None):
            return sb.tile(shape, dtype, name=name, tag=tag or name, align_bytes=64)

        def bank(name, shape, tag=None):
            return ps.tile(shape, F32, name=name, tag=tag or name)

        def load_words(name, words):
            window = tile(name, [P, T], U16)
            nc.sync.dma_start(window[:].bitcast(I32), words[0].bitcast(I32))
            return window

        def load_scale_rows(window, scales):
            for f in range(4):
                nc.sync.dma_start(window[f:P:32, :].bitcast(I32), scales[0, f:16:4, :].bitcast(I32))

        def load_rows(name, rows):
            raw = tile(name, [P, PACK, Q], F32)
            nc.sync.dma_start(raw[:], rows.rearrange("(p j) w -> p j w", j=PACK))
            return raw

        def interleave(name, raw):
            grouped = tile(name + "_bf16", [P, Q, PACK], BF16)
            nc.scalar.copy(
                grouped[:].rearrange("p (c i) t -> p c t i", i=4),
                raw[:].rearrange("p t (c i) -> p c t i", i=4),
            )
            return grouped

        def quantise(name, grouped):
            codes = tile(name + "_codes", [P, Q], U32)
            plane = tile(name + "_plane", [P, Q], U8)
            nc.vector.quantize_mx(codes[:].bitcast(FP8X4), plane[:], grouped[:].rearrange("p w t -> p (w t)"))
            return codes, plane

        def gather(name, window, dtype):
            picked = tile(name, [P, I], dtype)
            nc.vector.tensor_copy(picked[:], window[:].indirect(offsets[:]))
            return picked

        key_scale_window = tile("key_scale_window", [P, T], U8)
        val_scale_window = tile("val_scale_window", [P, T], U8)
        age_window = tile("age_window", [P, T], F32)
        nc.vector.memset(key_scale_window[:].bitcast(I32), 0)
        nc.vector.memset(age_window[0:AGE_ROW, :], 0.0)
        nc.vector.memset(val_scale_window[:].bitcast(I32), 0)

        rate_col = tile("rate_col", [P, 1], F32)
        nc.scalar.dma_start(rate_col[:], rate)
        size_cols = tile("size_cols", [P, 4], F32)
        nc.scalar.dma_start(size_cols[:], size[0].rearrange("(p j) -> p j", j=4))
        warm_in = tile("warm_in", [P, 1], F32)
        warm_out = tile("warm_out", [P, 1], F32)
        nc.gpsimd.memset(warm_in[:], 0.0)
        nc.scalar.activation(warm_out[:], warm_in[:], ACT.Exp)
        ident = tile("ident", [P, P], F32)
        make_identity(nc, ident[:])

        offsets = sb.tile([P, I // 16], U16, name="offsets")
        nc.sync.dma_start(offsets[:], offs)
        nc.sync.dma_start(age_window[AGE_ROW:P, :], age[0:1, :])
        key_window = load_words("key_window", keys_words)
        query_raw = load_rows("query_raw", query)
        load_scale_rows(key_scale_window, keys_scales)
        gout_raw = load_rows("gout_raw", gout)
        val_window = load_words("val_window", vals_words)
        load_scale_rows(val_scale_window, vals_scales)
        reserve_col = tile("reserve_col", [P, 1], F32)
        nc.sync.dma_start(reserve_col[:], reserve)
        base_sb = tile("base_sb", [P, I], F32)
        nc.sync.dma_start(base_sb[:], base)

        query_bf16 = interleave("query", query_raw)
        gout_bf16 = interleave("gout", gout_raw)

        age_picked = gather("age_picked", age_window, F32)
        rate_rows = bank("rate_rows", [P, Q])
        nc.tensor.transpose(rate_rows[:], rate_col[:].to_broadcast([P, P]), ident[:])
        age_turned = bank("age_turned", [P, BLOCKS, P])
        for j in range(BLOCKS):
            nc.tensor.transpose(age_turned[:, j, :], age_picked[:, j * P : (j + 1) * P], ident[:])
        size_rows = bank("size_rows", [P, 4, P])
        for j in range(4):
            nc.tensor.transpose(size_rows[:, j, :], size_cols[:, j : j + 1].to_broadcast([P, P]), ident[:])
        fade_and_age = tile("fade_and_age", [P, BLOCKS * Q + BLOCKS], F32, tag="query_raw")
        neg_age = fade_and_age[:, BLOCKS * Q :]
        fade_t = fade_and_age[:, : BLOCKS * Q].rearrange("s (j q) -> s j q", j=BLOCKS)
        nc.scalar.activation(neg_age, age_turned[:, :, AGE_ROW], ACT.Copy, scale=-1.0)
        for j in range(BLOCKS):
            nc.scalar.activation(fade_t[:, j, :], rate_rows[:], ACT.Copy, scale=neg_age[:, j : j + 1])
        exponent = [bank("exponent%d" % h, [P, 2, P]) for h in range(2)]
        for j in range(BLOCKS):
            nc.tensor.matmul(
                exponent[j // 2][:, j % 2, :], fade_t[:, j, :], ident[:], start=(j % 2 == 0), stop=False, is_transpose=True
            )

        key_words = gather("key_words", key_window, U16)
        query_codes, query_plane = quantise("query", query_bf16)
        key_plane = tile("key_plane", [P, I], U8, tag="query_bf16")
        score_t = tile("score_t", [P, BLOCKS, Q], F32, tag="gout_raw")
        p = tile("p", [P, I], F32)
        z = reserve_col
        for h in range(2):
            half = slice(h * HALF, (h + 1) * HALF)
            nc.vector.tensor_copy(
                key_plane[:, half], key_scale_window[:].indirect(offsets[:, h * HALF // 16 : (h + 1) * HALF // 16])
            )
            score_bank = bank("score_bank%d" % h, [P, 2, Q])
            for u in range(2):
                cols = slice((2 * h + u) * P, (2 * h + u + 1) * P)
                nc.tensor.matmul_mx(
                    score_bank[:, u, :],
                    lhsT=key_words[:, cols].bitcast(FP4X4),
                    lhsT_scale=key_plane[:, cols],
                    rhs=query_codes[:].bitcast(FP8X4),
                    rhs_scale=query_plane[:],
                    start=True,
                    stop=True,
                )
            nc.scalar.copy(score_t[:, 2 * h : 2 * h + 2, :], score_bank[:])
            for u in range(2):
                nc.tensor.matmul(
                    exponent[h][:, u, :], score_t[:, 2 * h + u, :], ident[:], start=False, stop=(u == 1), is_transpose=True
                )
            p_sum = tile("p_sum%d" % h, [P, 1], F32)
            nc.scalar.activation(p[:, half], exponent[h][:].rearrange("q j s -> q (j s)"), ACT.Exp, accum_out=p_sum[:])
            z_next = tile("z%d" % h, [P, 1], F32)
            nc.scalar.activation(z_next[:], p_sum[:], ACT.Identity, bias=z[:])
            z = z_next

        val_words = gather("val_words", val_window, U16)
        gout_codes, gout_plane = quantise("gout", gout_bf16)
        val_plane = gather("val_plane", val_scale_window, U8)
        c0 = bank("c0", [P, I], tag="exponent1")
        nc.tensor.matmul_mx(
            c0[:],
            lhsT=gout_codes[:].bitcast(FP8X4),
            lhsT_scale=gout_plane[:],
            rhs=val_words[:].bitcast(FP4X4),
            rhs_scale=val_plane[:],
            start=True,
            stop=True,
        )

        p_size_and_r = tile("p_size_and_r", [P, I + 1], F32, tag="val_scale_window")
        p_size = p_size_and_r[:, :I]
        r = p_size_and_r[:, I:]
        nc.vector.tensor_tensor(
            p_size.rearrange("q (s j) -> q s j", j=4),
            p[:].rearrange("q (s j) -> q s j", j=4),
            size_rows[:].rearrange("q j s -> q s j"),
            ALU.mult,
        )
        nc.vector.reciprocal(r, z[:])
        s = tile("s", [P, I], F32)
        nc.scalar.activation(s[:], p[:], ACT.Copy, scale=r)
        v = tile("v", [P, I], F32)
        v_sum = tile("v_sum", [P, 1], F32)
        nc.vector.scalar_tensor_tensor(v[:], p_size, r, c0[:], ALU.mult, ALU.mult, accum_out=v_sum[:])
        t = tile("t", [P, I], F32)
        nc.vector.scalar_tensor_tensor(t[:], s[:], v_sum[:], v[:], ALU.mult, ALU.subtract)
        squares = tile("squares", [P, I], F32)
        square_sum = tile("square_sum", [P, 1], F32)
        nc.scalar.activation(squares[:], t[:], ACT.Square, scale=ROOT_K, accum_out=square_sum[:])
        cross = tile("cross", [P, I], F32)
        shift = tile("shift", [P, 1], F32)
        nc.vector.scalar_tensor_tensor(cross[:], t[:], -0.5 * ROOT_K, s[:], ALU.mult, ALU.mult, accum_out=shift[:])
        halves = [slice(h * HALF, (h + 1) * HALF) for h in range(2)]
        linear = tile("linear", [P, I], F32)
        for half in halves:
            nc.vector.scalar_tensor_tensor(
                linear[:, half], s[:, half], square_sum[:], base_sb[:, half], ALU.mult, ALU.subtract
            )
        shift_sq = tile("shift_sq", [P, 1], F32)
        nc.scalar.activation(shift_sq[:], shift[:], ACT.Square)
        shifted = tile("shifted", [P, I], F32)
        result = tile("result", [P, I], F32)
        for half in halves:
            nc.scalar.activation(shifted[:, half], t[:, half], ACT.Square, scale=ROOT_K, bias=shift[:])
            nc.vector.scalar_tensor_tensor(
                result[:, half], shifted[:, half], shift_sq[:], linear[:, half], ALU.subtract, ALU.subtract
            )
            nc.sync.dma_start(out[:, half], result[:, half])
